import numpy as np
import ml_dtypes


def mxq(x, axis, fmt="e4m3"):
    dtype, down = {"e4m3": (ml_dtypes.float8_e4m3fn, 7), "e5m2": (ml_dtypes.float8_e5m2, 14)}[fmt]
    v = np.moveaxis(np.asarray(x, np.float32).astype(ml_dtypes.bfloat16).astype(np.float64), axis, -1)
    blocks = v.reshape(v.shape[:-1] + (-1, 32))
    amax = np.abs(blocks).max(-1, keepdims=True)
    byte = np.maximum(np.where(amax > 0, np.frexp(amax)[1] - 1 + 127, 0) - down, 1)
    scale = np.exp2(byte - 127.0)
    codes = (blocks / scale).astype(np.float32).astype(dtype).astype(np.float64)
    return np.moveaxis((codes * scale).reshape(v.shape), -1, axis)


WIDE = False


def mx_kscale(k):
    if not WIDE:
        return np.ones(k)
    levels = np.array([10, -10, 5, -5, 0])
    if k % 512:
        return np.exp2(np.random.permutation(np.resize(levels, k // 32))).repeat(32)
    a = np.empty((k // 512, 16))
    for p in range(k // 512):
        a[p, :8] = np.random.permutation(np.resize(levels, 8))
        for g in range(8):
            far = levels[np.abs(levels - a[p, g]) >= 10]
            a[p, g + 8] = far[np.random.randint(len(far))]
    return np.exp2(a.ravel()).repeat(32)


def f64(x):
    return np.asarray(x).astype(np.float64)


def striped(idx):
    return np.tile(idx.reshape(-1, 16).T, (8, 1)).astype(np.uint16)


def unstriped(offs):
    return offs[:16].T.reshape(-1).astype(np.int64)


E2M1 = np.array([0.0, 0.5, 1.0, 1.5, 2.0, 3.0, 4.0, 6.0, -0.0, -0.5, -1.0, -1.5, -2.0, -3.0, -4.0, -6.0])


def pack_weight(w, fmt):
    k, n = w.shape
    w = f64(np.asarray(w, np.float32).astype(ml_dtypes.bfloat16)).reshape(k // 32, 32, n)
    amax = np.abs(w).max(1)
    if fmt == "e4m3":
        byte = np.frexp(amax)[1] - 1 + 127 - 7
    else:
        mant, ex = np.frexp(amax / 6.0)
        byte = np.where(mant > 0.5, ex, ex - 1) + 127
    byte = np.clip(np.where(amax > 0, byte, 1), 1, 254)
    scaled = (w * np.exp2(127.0 - byte)[:, None, :]).reshape(k, n).astype(np.float32)
    by_word = np.ascontiguousarray(scaled.reshape(k // 512, 128, 4, n).transpose(0, 1, 3, 2))
    if fmt == "e4m3":
        words = by_word.astype(ml_dtypes.float8_e4m3fn).view(np.uint8)
    else:
        c = by_word.astype(ml_dtypes.float4_e2m1fn).view(np.uint8) & 0xF
        words = (c[..., 0::2] | (c[..., 1::2] << 4)).reshape(k // 512, 128, 2 * n)
    return np.ascontiguousarray(words), np.ascontiguousarray(byte.astype(np.uint8).reshape(k // 512, 16, n))


def unpack_weight(words, scales, fmt):
    g, _, n = scales.shape
    words = np.ascontiguousarray(words).reshape(g, 128, n, -1)
    if fmt == "e4m3":
        vals = words.view(ml_dtypes.float8_e4m3fn).astype(np.float64)
    else:
        nib = np.empty((g, 128, n, 4), np.uint8)
        nib[..., 0::2] = words & 0xF
        nib[..., 1::2] = words >> 4
        vals = E2M1[nib]
    vals = vals * np.repeat(np.exp2(scales.astype(np.float64) - 127.0), 8, axis=1)[..., None]
    return vals.transpose(0, 1, 3, 2).reshape(g * 512, n)


def pack_table(v):
    words, scales = pack_weight(v, "e4m3")
    return np.concatenate([words.reshape(words.shape[0], -1), scales.reshape(scales.shape[0], -1)], axis=1)


def unpack_table(tab):
    g, t = tab.shape[0], tab.shape[1] // 528
    return unpack_weight(tab[:, :512 * t].reshape(g, 128, t, 4), tab[:, 512 * t:].reshape(g, 16, t), "e4m3")


def silu(v):
    return v / (1.0 + np.exp(-np.maximum(v, -700.0)))


K, M, T, S = 2048, 1024, 4096, 1024


def setup_inputs():
    n = np.random.standard_normal
    s = mx_kscale(K)[:, None]
    p_w4 = pack_weight(n((K, M)) / np.sqrt(K) / s, "e2m1")
    return {
        "tab": pack_table(n((K, T)) * s),
        "w4_words": p_w4[0],
        "w4_scales": p_w4[1],
        "w8": (n((K, M)) / np.sqrt(K) / s).astype(np.float32),
        "offs": striped(np.random.permutation(T)[:S]),
    }


def reference(tab, w4_words, w4_scales, w8, offs):
    tab_ = unpack_table(tab)[:, unstriped(offs)]
    w4_ = unpack_weight(w4_words, w4_scales, "e2m1")
    w8_ = mxq(f64(w8), 0, "e4m3")
    y = tab_.T @ w4_
    u = tab_.T @ w8_
    y = silu(y) * u
    return y

@@ -1,0 +1,241 @@
+from contextlib import ExitStack
+
+import concourse.mybir as mybir
+
+K, M, T, S = 2048, 1024, 4096, 1024
+FLOPS = 2 * 2 * K * M * S
+
+F32 = mybir.dt.float32
+BF16 = mybir.dt.bfloat16
+I32 = mybir.dt.int32
+U32 = mybir.dt.uint32
+U16 = mybir.dt.uint16
+U8 = mybir.dt.uint8
+FP8X4 = mybir.dt.float8_e4m3fn_x4
+FP4X4 = mybir.dt.float4_e2m1fn_x4
+SILU = mybir.ActivationFunctionType.Silu
+MULT = mybir.AluOpType.mult
+
+P = 128
+PASSES = K // 512
+HALF = 512
+TOKENS = S // P
+KIB = 1024
+TABLE_AT = [16 * KIB, 32 * KIB, 0, 16 * KIB]
+W4_AT = 32 * KIB
+RAW_AT = [40 * KIB, 0, 8 * KIB, 16 * KIB, 24 * KIB, 40 * KIB, 0, 8 * KIB]
+SCALAR_COLUMNS = [0, 0, 0, 0, 320, 320, 320, 320]
+
+
+def tile_list_tabglu_tm_none_kernel(tc, tab, w4_words, w4_scales, w8, offs, out):
+    nc = tc.nc
+    words_bytes = 512 * T
+
+    with ExitStack() as ctx:
+        keep = ctx.enter_context(tc.tile_pool(name="keep", bufs=1))
+        shared = ctx.enter_context(tc.tile_pool(name="shared", bufs=1))
+        stage = ctx.enter_context(tc.tile_pool(name="stage", bufs=3))
+        outs = ctx.enter_context(tc.tile_pool(name="outs", bufs=4))
+        psum = ctx.enter_context(tc.psum_pool(name="psum", bufs=8))
+
+        offsets = keep.tile([P, S // 16], U16, name="offsets")
+        nc.sync.dma_start(offsets[:], offs)
+
+        table_scales = shared.tile([P, T // 4], I32, align_bytes=64, offset=TABLE_AT[2], name="table_scales")
+        w4_planes = keep.tile([P, PASSES * M // 4], I32, align_bytes=64, name="w4_planes")
+        moved = keep.tile([P, (PASSES - 1) * S // 4], I32, align_bytes=64, name="moved")
+        nc.vector.memset(table_scales[:], 0)
+        nc.gpsimd.memset(moved[:], 0)
+
+        warm = keep.tile([P, 1], F32, name="warm")
+        nc.gpsimd.memset(warm[:], 0.0)
+        warm_out = keep.tile([P, 1], F32, name="warm_out")
+        nc.scalar.activation(warm_out[:], warm[:], SILU)
+
+        table = {}
+        w4_codes = {}
+
+        def load_table(a):
+            offset = TABLE_AT[a]
+            table[a] = shared.tile([P, T], I32, align_bytes=64, offset=offset, name=f"table{a}")
+            if a == 0:
+                nc.vector.memset(table[a][:, 0:16], 0)
+                nc.vector.memset(w4_planes[:], 0)
+            if a == 1:
+                nc.vector.memset(table[a][:, 0:16], 0)
+            nc.sync.dma_start(table[a][:], tab[a, 0:words_bytes].rearrange("(p x) -> p x", p=P).bitcast(I32))
+
+        def load_w4(a0, a1, h):
+            shape = [P, a1 - a0, HALF // 2]
+            if (a0, h) == (0, 0):
+                tile = keep.tile(shape, I32, align_bytes=64, name="w4_first")
+            else:
+                tile = shared.tile(shape, I32, align_bytes=64, offset=W4_AT + h * 2 * HALF, name=f"w4_{a0}{h}")
+            nc.sync.dma_start(
+                tile[:], w4_words[a0:a1, :, h * 2 * HALF : (h + 1) * 2 * HALF].rearrange("a p x -> p a x").bitcast(I32)
+            )
+            for a in range(a0, a1):
+                w4_codes[a, h] = tile[:, a - a0, :]
+
+        def load_w8(a, h):
+            i = h * PASSES + a
+            raw = shared.tile([P, 4, HALF], F32, align_bytes=64, offset=RAW_AT[i], name=f"raw{i}")
+            nc.sync.dma_start(
+                raw[:],
+                w8[512 * a : 512 * (a + 1), h * HALF : (h + 1) * HALF].rearrange("(p j) n -> p j n", j=4),
+            )
+            return raw
+
+        load_w4(0, 3, 0)
+        for q in range(4):
+            nc.sync.dma_start(
+                table_scales[32 * q : 32 * q + 16, :],
+                tab[:, words_bytes + 4 * q * T : words_bytes + (4 * q + 4) * T]
+                .rearrange("a (r t) -> a r t", r=4)
+                .bitcast(I32),
+            )
+        load_table(0)
+        for q in range(4):
+            nc.sync.dma_start(
+                w4_planes[32 * q : 32 * q + 4, :].rearrange("r (a n) -> r a n", a=PASSES),
+                w4_scales[:, 4 * q : 4 * q + 4, :].rearrange("a r n -> r a n").bitcast(I32),
+            )
+        load_table(1)
+        picked_scales = keep.tile([P, S], U8, align_bytes=64, name="picked_scales")
+        nc.vector.tensor_copy(picked_scales[:], table_scales[:].bitcast(U8).indirect(offsets[:]))
+        for a in range(1, PASSES):
+            nc.scalar.dma_start(
+                moved[0 : P - 4 * a, (a - 1) * S // 4 : a * S // 4], picked_scales[4 * a : P, :].bitcast(I32)
+            )
+        load_table(2)
+        order = [(a, h) for h in range(2) for a in range(PASSES)]
+        raw_of = {}
+
+        picked = [keep.tile([P, S], U32, align_bytes=64, name=f"picked{a}") for a in range(PASSES)]
+
+        def gather_words(a, parts=1):
+            n = S // parts
+            for i in range(parts):
+                nc.vector.tensor_copy(
+                    picked[a][:, i * n : (i + 1) * n],
+                    table[a][:].bitcast(U32).indirect(offsets[:, i * n // 16 : (i + 1) * n // 16]),
+                )
+
+        moved_u8 = moved[:].bitcast(U8)
+        w4_planes_u8 = w4_planes[:].bitcast(U8)
+
+        def token_operand(a, t):
+            cols = slice(t * P, (t + 1) * P)
+            codes = picked[a][:, cols].bitcast(FP8X4)
+            if a == 0:
+                return codes, picked_scales[:, cols]
+            return codes, moved_u8[:, (a - 1) * S + t * P : (a - 1) * S + (t + 1) * P]
+
+        def mm_w4(acc, a, t, h):
+            codes, scales = token_operand(a, t)
+            nc.tensor.matmul_mx(
+                out=acc[:],
+                lhsT=codes,
+                lhsT_scale=scales,
+                rhs=w4_codes[a, h].bitcast(U8).bitcast(FP4X4),
+                rhs_scale=w4_planes_u8[:, a * M + h * HALF : a * M + (h + 1) * HALF],
+                start=(a == 0),
+                stop=(a == PASSES - 1),
+            )
+
+        w8_codes = {}
+
+        def quantize_w8(i):
+            a, h = order[i]
+            raw = raw_of[a, h]
+            cut = SCALAR_COLUMNS[i]
+            grouped = stage.tile([P, HALF, 4], BF16, align_bytes=64, name="grouped")
+            dst = grouped[:].rearrange("p (c i) t -> p c t i", i=4)
+            src = raw[:].rearrange("p t (c i) -> p c t i", i=4)
+            if cut:
+                nc.scalar.copy(dst[:, : cut // 4], src[:, : cut // 4])
+            nc.vector.tensor_copy(dst[:, cut // 4 :], src[:, cut // 4 :])
+            codes = keep.tile([P, HALF], U32, align_bytes=64, name=f"w8_codes{a}{h}")
+            scales = keep.tile([P, HALF], U8, align_bytes=64, name=f"w8_scales{a}{h}")
+            nc.vector.quantize_mx(
+                out=codes[:].bitcast(FP8X4), scales=scales[:], in_=grouped[:].rearrange("p n t -> p (n t)")
+            )
+            w8_codes[a, h] = (codes, scales)
+
+        def mm_w8(acc, a, t, h):
+            codes, scales = token_operand(a, t)
+            w_codes, w_scales = w8_codes[a, h]
+            nc.tensor.matmul_mx(
+                out=acc[:],
+                lhsT=codes,
+                lhsT_scale=scales,
+                rhs=w_codes[:].bitcast(FP8X4),
+                rhs_scale=w_scales[:],
+                start=(a == 0),
+                stop=(a == PASSES - 1),
+            )
+
+        gates = {}
+
+        def gate(acc, t, h):
+            g = keep.tile([P, HALF], F32, name=f"gate{t}{h}")
+            nc.scalar.activation(g[:], acc[:], SILU)
+            gates[t, h] = g
+
+        def load_raw(i):
+            raw_of[order[i]] = load_w8(*order[i])
+
+        accs = [psum.tile([P, HALF], F32, name="acc") for t in range(TOKENS)]
+        for a in range(PASSES):
+            gather_words(a, 2 if a == PASSES - 1 else 1)
+            if a == 0:
+                load_table(3)
+            for t in range(TOKENS):
+                mm_w4(accs[t], a, t, 0)
+            if a == 1:
+                load_w4(3, 4, 0)
+                load_w4(0, 4, 1)
+                load_raw(0)
+            if a == 2:
+                load_raw(1)
+                load_raw(2)
+            if a == 3:
+                load_raw(3)
+                load_raw(4)
+        for t in range(TOKENS):
+            gate(accs[t], t, 0)
+
+        def prepare(unit):
+            if unit >= 2 and unit % 2 == 0 and unit <= 16:
+                i = (unit - 2) // 2
+                quantize_w8(i)
+                if i < 3:
+                    load_raw(i + 5)
+
+        for t in range(TOKENS):
+            prepare(t)
+            acc = psum.tile([P, HALF], F32, name="acc")
+            for a in range(PASSES):
+                mm_w4(acc, a, t, 1)
+            gate(acc, t, 1)
+
+        waiting = []
+
+        def finish():
+            acc, t, h = waiting.pop(0)
+            mm_w8(acc, PASSES - 1, t, h)
+            res = outs.tile([P, HALF], F32, name="res")
+            nc.vector.tensor_tensor(res[:], acc[:], gates[t, h][:], MULT)
+            nc.sync.dma_start(out[t * P : (t + 1) * P, h * HALF : (h + 1) * HALF], res[:])
+
+        for h in range(2):
+            for t in range(TOKENS):
+                prepare(TOKENS * (h + 1) + t)
+                acc = psum.tile([P, HALF], F32, name="acc")
+                for a in range(PASSES - 1):
+                    mm_w8(acc, a, t, h)
+                waiting.append((acc, t, h))
+                if len(waiting) > 2:
+                    finish()
+        while waiting:
+            finish()

@@ -21,10 +21,12 @@ PASSES = K // 512
 HALF = 512
 TOKENS = S // P
 KIB = 1024
-TABLE_AT = [16 * KIB, 32 * KIB, 0, 16 * KIB]
-W4_AT = 32 * KIB
-RAW_AT = [40 * KIB, 0, 8 * KIB, 16 * KIB, 24 * KIB, 40 * KIB, 0, 8 * KIB]
-SCALAR_COLUMNS = [0, 0, 0, 0, 320, 320, 320, 320]
+TABLE_AT = [15 * KIB, 48 * KIB, 0, 17 * KIB]
+PICKED_SCALES_AT = 16 * KIB
+W4_LATE_AT = [48 * KIB, 49 * KIB]
+PLANES_LATE_AT = 53 * KIB
+RAW_AT = {(0, None): 55 * KIB, (1, None): 0, (2, None): 17 * KIB, (3, 0): 55 * KIB, (3, 1): 63 * KIB}
+SCALAR_COLUMNS = {(3, 0): 256, (3, 1): 384}
 
 
 def tile_list_tabglu_tm_none_kernel(tc, tab, w4_words, w4_scales, w8, offs, out):
@@ -34,83 +36,61 @@ def tile_list_tabglu_tm_none_kernel(tc, tab, w4_words, w4_scales, w8, offs, out)
     with ExitStack() as ctx:
         keep = ctx.enter_context(tc.tile_pool(name="keep", bufs=1))
         shared = ctx.enter_context(tc.tile_pool(name="shared", bufs=1))
-        stage = ctx.enter_context(tc.tile_pool(name="stage", bufs=3))
-        outs = ctx.enter_context(tc.tile_pool(name="outs", bufs=4))
+        stage = ctx.enter_context(tc.tile_pool(name="stage", bufs=5))
+        outs = ctx.enter_context(tc.tile_pool(name="outs", bufs=6))
         psum = ctx.enter_context(tc.psum_pool(name="psum", bufs=8))
 
         offsets = keep.tile([P, S // 16], U16, name="offsets")
         nc.sync.dma_start(offsets[:], offs)
 
-        table_scales = shared.tile([P, T // 4], I32, align_bytes=64, offset=TABLE_AT[2], name="table_scales")
-        w4_planes = keep.tile([P, PASSES * M // 4], I32, align_bytes=64, name="w4_planes")
-        moved = keep.tile([P, (PASSES - 1) * S // 4], I32, align_bytes=64, name="moved")
-        nc.vector.memset(table_scales[:], 0)
-        nc.gpsimd.memset(moved[:], 0)
-
         warm = keep.tile([P, 1], F32, name="warm")
         nc.gpsimd.memset(warm[:], 0.0)
         warm_out = keep.tile([P, 1], F32, name="warm_out")
         nc.scalar.activation(warm_out[:], warm[:], SILU)
+        moved = keep.tile([P, (PASSES - 1) * S // 4], I32, align_bytes=64, name="moved")
+        nc.gpsimd.memset(moved[:], 0)
 
-        table = {}
         w4_codes = {}
+        w4_planes = {}
 
-        def load_table(a):
-            offset = TABLE_AT[a]
-            table[a] = shared.tile([P, T], I32, align_bytes=64, offset=offset, name=f"table{a}")
-            if a == 0:
-                nc.vector.memset(table[a][:, 0:16], 0)
-                nc.vector.memset(w4_planes[:], 0)
-            if a == 1:
-                nc.vector.memset(table[a][:, 0:16], 0)
-            nc.sync.dma_start(table[a][:], tab[a, 0:words_bytes].rearrange("(p x) -> p x", p=P).bitcast(I32))
-
-        def load_w4(a0, a1, h):
-            shape = [P, a1 - a0, HALF // 2]
-            if (a0, h) == (0, 0):
-                tile = keep.tile(shape, I32, align_bytes=64, name="w4_first")
-            else:
-                tile = shared.tile(shape, I32, align_bytes=64, offset=W4_AT + h * 2 * HALF, name=f"w4_{a0}{h}")
+        def load_w4(tile, a0, a1, h):
             nc.sync.dma_start(
                 tile[:], w4_words[a0:a1, :, h * 2 * HALF : (h + 1) * 2 * HALF].rearrange("a p x -> p a x").bitcast(I32)
             )
             for a in range(a0, a1):
                 w4_codes[a, h] = tile[:, a - a0, :]
 
-        def load_w8(a, h):
-            i = h * PASSES + a
-            raw = shared.tile([P, 4, HALF], F32, align_bytes=64, offset=RAW_AT[i], name=f"raw{i}")
-            nc.sync.dma_start(
-                raw[:],
-                w8[512 * a : 512 * (a + 1), h * HALF : (h + 1) * HALF].rearrange("(p j) n -> p j n", j=4),
-            )
-            return raw
+        def load_planes(engine, tile, h):
+            for q in range(4):
+                engine.dma_start(
+                    tile[32 * q : 32 * q + 4, :, :],
+                    w4_scales[:, 4 * q : 4 * q + 4, h * HALF : (h + 1) * HALF].rearrange("a r n -> r a n").bitcast(I32),
+                )
+            for a in range(PASSES):
+                w4_planes[a, h] = tile[:, a, :].bitcast(U8)
 
-        load_w4(0, 3, 0)
+        table = {}
+
+        def load_table(a):
+            table[a] = shared.tile([P, T], I32, align_bytes=64, offset=TABLE_AT[a], name=f"table{a}")
+            nc.sync.dma_start(table[a][:], tab[a, 0:words_bytes].rearrange("(p x) -> p x", p=P).bitcast(I32))
+
+        load_table(0)
+        w4_first = keep.tile([P, PASSES - 1, HALF // 2], I32, align_bytes=64, name="w4_first")
+        load_w4(w4_first, 0, PASSES - 1, 0)
+        table_scales = keep.tile([P, T // 4], I32, align_bytes=64, name="table_scales")
+        nc.vector.memset(table_scales[:], 0)
         for q in range(4):
-            nc.sync.dma_start(
+            nc.gpsimd.dma_start(
                 table_scales[32 * q : 32 * q + 16, :],
                 tab[:, words_bytes + 4 * q * T : words_bytes + (4 * q + 4) * T]
                 .rearrange("a (r t) -> a r t", r=4)
                 .bitcast(I32),
             )
-        load_table(0)
-        for q in range(4):
-            nc.sync.dma_start(
-                w4_planes[32 * q : 32 * q + 4, :].rearrange("r (a n) -> r a n", a=PASSES),
-                w4_scales[:, 4 * q : 4 * q + 4, :].rearrange("a r n -> r a n").bitcast(I32),
-            )
+        planes_first = keep.tile([P, PASSES, HALF // 4], I32, align_bytes=64, name="planes_first")
+        nc.vector.memset(planes_first[:], 0)
+        load_planes(nc.sync, planes_first, 0)
         load_table(1)
-        picked_scales = keep.tile([P, S], U8, align_bytes=64, name="picked_scales")
-        nc.vector.tensor_copy(picked_scales[:], table_scales[:].bitcast(U8).indirect(offsets[:]))
-        for a in range(1, PASSES):
-            nc.scalar.dma_start(
-                moved[0 : P - 4 * a, (a - 1) * S // 4 : a * S // 4], picked_scales[4 * a : P, :].bitcast(I32)
-            )
-        load_table(2)
-        order = [(a, h) for h in range(2) for a in range(PASSES)]
-        raw_of = {}
-
         picked = [keep.tile([P, S], U32, align_bytes=64, name=f"picked{a}") for a in range(PASSES)]
 
         def gather_words(a, parts=1):
@@ -121,8 +101,17 @@ def tile_list_tabglu_tm_none_kernel(tc, tab, w4_words, w4_scales, w8, offs, out)
                     table[a][:].bitcast(U32).indirect(offsets[:, i * n // 16 : (i + 1) * n // 16]),
                 )
 
+        gather_words(0)
+        picked_scales = shared.tile([P, S], U8, align_bytes=64, offset=PICKED_SCALES_AT, name="picked_scales")
+        nc.vector.tensor_copy(picked_scales[:], table_scales[:].bitcast(U8).indirect(offsets[:]))
+        for a in range(1, PASSES):
+            nc.scalar.dma_start(
+                moved[0:112, (a - 1) * S // 4 : a * S // 4], picked_scales[4 * a : 4 * a + 112, :].bitcast(I32)
+            )
+        load_table(2)
+        load_table(3)
+
         moved_u8 = moved[:].bitcast(U8)
-        w4_planes_u8 = w4_planes[:].bitcast(U8)
 
         def token_operand(a, t):
             cols = slice(t * P, (t + 1) * P)
@@ -131,27 +120,45 @@ def tile_list_tabglu_tm_none_kernel(tc, tab, w4_words, w4_scales, w8, offs, out)
                 return codes, picked_scales[:, cols]
             return codes, moved_u8[:, (a - 1) * S + t * P : (a - 1) * S + (t + 1) * P]
 
-        def mm_w4(acc, a, t, h):
+        def multiply(acc, a, t, rhs, rhs_scale):
             codes, scales = token_operand(a, t)
             nc.tensor.matmul_mx(
                 out=acc[:],
                 lhsT=codes,
                 lhsT_scale=scales,
-                rhs=w4_codes[a, h].bitcast(U8).bitcast(FP4X4),
-                rhs_scale=w4_planes_u8[:, a * M + h * HALF : a * M + (h + 1) * HALF],
+                rhs=rhs,
+                rhs_scale=rhs_scale,
                 start=(a == 0),
                 stop=(a == PASSES - 1),
             )
 
+        def mm_w4(acc, a, t, h):
+            multiply(acc, a, t, w4_codes[a, h].bitcast(U8).bitcast(FP4X4), w4_planes[a, h])
+
         w8_codes = {}
 
-        def quantize_w8(i):
-            a, h = order[i]
-            raw = raw_of[a, h]
-            cut = SCALAR_COLUMNS[i]
+        def mm_w8(acc, a, t, h):
+            codes, scales = w8_codes[a, h]
+            multiply(acc, a, t, codes[:].bitcast(FP8X4), scales[:])
+
+        raws = {}
+
+        def load_w8(a, half):
+            if half is None:
+                cols, key = slice(0, M), f"raw{a}"
+            else:
+                cols, key = slice(half * HALF, (half + 1) * HALF), f"raw{a}{half}"
+            width = cols.stop - cols.start
+            raw = shared.tile([P, 4, width], F32, align_bytes=64, offset=RAW_AT[a, half], name=key)
+            nc.sync.dma_start(raw[:], w8[512 * a : 512 * (a + 1), cols].rearrange("(p j) n -> p j n", j=4))
+            for h in range(2) if half is None else [half]:
+                raws[a, h] = raw[:, :, h * HALF : (h + 1) * HALF] if half is None else raw[:]
+
+        def quantize_w8(a, h):
+            cut = SCALAR_COLUMNS.get((a, h), 0)
             grouped = stage.tile([P, HALF, 4], BF16, align_bytes=64, name="grouped")
             dst = grouped[:].rearrange("p (c i) t -> p c t i", i=4)
-            src = raw[:].rearrange("p t (c i) -> p c t i", i=4)
+            src = raws[a, h].rearrange("p t (c i) -> p c t i", i=4)
             if cut:
                 nc.scalar.copy(dst[:, : cut // 4], src[:, : cut // 4])
             nc.vector.tensor_copy(dst[:, cut // 4 :], src[:, cut // 4 :])
@@ -162,19 +169,6 @@ def tile_list_tabglu_tm_none_kernel(tc, tab, w4_words, w4_scales, w8, offs, out)
             )
             w8_codes[a, h] = (codes, scales)
 
-        def mm_w8(acc, a, t, h):
-            codes, scales = token_operand(a, t)
-            w_codes, w_scales = w8_codes[a, h]
-            nc.tensor.matmul_mx(
-                out=acc[:],
-                lhsT=codes,
-                lhsT_scale=scales,
-                rhs=w_codes[:].bitcast(FP8X4),
-                rhs_scale=w_scales[:],
-                start=(a == 0),
-                stop=(a == PASSES - 1),
-            )
-
         gates = {}
 
         def gate(acc, t, h):
@@ -182,60 +176,70 @@ def tile_list_tabglu_tm_none_kernel(tc, tab, w4_words, w4_scales, w8, offs, out)
             nc.scalar.activation(g[:], acc[:], SILU)
             gates[t, h] = g
 
-        def load_raw(i):
-            raw_of[order[i]] = load_w8(*order[i])
-
-        accs = [psum.tile([P, HALF], F32, name="acc") for t in range(TOKENS)]
-        for a in range(PASSES):
-            gather_words(a, 2 if a == PASSES - 1 else 1)
-            if a == 0:
-                load_table(3)
-            for t in range(TOKENS):
-                mm_w4(accs[t], a, t, 0)
-            if a == 1:
-                load_w4(3, 4, 0)
-                load_w4(0, 4, 1)
-                load_raw(0)
-            if a == 2:
-                load_raw(1)
-                load_raw(2)
-            if a == 3:
-                load_raw(3)
-                load_raw(4)
-        for t in range(TOKENS):
-            gate(accs[t], t, 0)
-
-        def prepare(unit):
-            if unit >= 2 and unit % 2 == 0 and unit <= 16:
-                i = (unit - 2) // 2
-                quantize_w8(i)
-                if i < 3:
-                    load_raw(i + 5)
-
-        for t in range(TOKENS):
-            prepare(t)
-            acc = psum.tile([P, HALF], F32, name="acc")
-            for a in range(PASSES):
-                mm_w4(acc, a, t, 1)
-            gate(acc, t, 1)
-
-        waiting = []
-
-        def finish():
-            acc, t, h = waiting.pop(0)
+        def finish(acc, t, h):
             mm_w8(acc, PASSES - 1, t, h)
             res = outs.tile([P, HALF], F32, name="res")
             nc.vector.tensor_tensor(res[:], acc[:], gates[t, h][:], MULT)
             nc.sync.dma_start(out[t * P : (t + 1) * P, h * HALF : (h + 1) * HALF], res[:])
 
-        for h in range(2):
+        accs = [psum.tile([P, HALF], F32, name="acc") for t in range(TOKENS)]
+        for a in range(PASSES):
+            if a > 0:
+                gather_words(a, 2 if a == PASSES - 1 else 1)
             for t in range(TOKENS):
-                prepare(TOKENS * (h + 1) + t)
-                acc = psum.tile([P, HALF], F32, name="acc")
-                for a in range(PASSES - 1):
-                    mm_w8(acc, a, t, h)
-                waiting.append((acc, t, h))
-                if len(waiting) > 2:
-                    finish()
+                mm_w4(accs[t], a, t, 0)
+            if a == 1:
+                w4_late0 = shared.tile([P, 1, HALF // 2], I32, align_bytes=64, offset=W4_LATE_AT[0], name="w4_late0")
+                load_w4(w4_late0, 3, 4, 0)
+                w4_late1 = shared.tile([P, PASSES, HALF // 2], I32, align_bytes=64, offset=W4_LATE_AT[1], name="w4_late1")
+                load_w4(w4_late1, 0, 4, 1)
+                planes_late = shared.tile(
+                    [P, PASSES, HALF // 4], I32, align_bytes=64, offset=PLANES_LATE_AT, name="planes_late"
+                )
+                nc.vector.memset(planes_late[:], 0)
+                load_planes(nc.sync, planes_late, 1)
+                load_w8(0, None)
+            if a == 2:
+                load_w8(1, None)
+            if a == 3:
+                load_w8(2, None)
+        for t in range(TOKENS):
+            gate(accs[t], t, 0)
+
+        for t in range(TOKENS):
+            if t == 3:
+                quantize_w8(0, 0)
+                quantize_w8(0, 1)
+                load_w8(3, 0)
+                load_w8(3, 1)
+            if t == 7:
+                quantize_w8(1, 0)
+                quantize_w8(1, 1)
+            acc = psum.tile([P, HALF], F32, name="acc")
+            for a in range(PASSES):
+                mm_w4(acc, a, t, 1)
+            gate(acc, t, 1)
+
+        accs = [psum.tile([P, HALF], F32, name="acc") for t in range(TOKENS)]
+        for a in range(PASSES - 1):
+            if a == 2:
+                quantize_w8(2, 0)
+                quantize_w8(2, 1)
+                quantize_w8(3, 0)
+            for t in range(TOKENS):
+                mm_w8(accs[t], a, t, 0)
+        for t in range(TOKENS):
+            finish(accs[t], t, 0)
+            if t == 1:
+                quantize_w8(3, 1)
+
+        waiting = []
+        for t in range(TOKENS):
+            acc = psum.tile([P, HALF], F32, name="acc")
+            for a in range(PASSES - 1):
+                mm_w8(acc, a, t, 1)
+            waiting.append((acc, t))
+            if len(waiting) > 2:
+                finish(*waiting.pop(0), 1)
         while waiting:
-            finish()
+            finish(*waiting.pop(0), 1)

@@ -25,8 +25,17 @@ TABLE_AT = [15 * KIB, 48 * KIB, 0, 17 * KIB]
 PICKED_SCALES_AT = 16 * KIB
 W4_LATE_AT = [48 * KIB, 49 * KIB]
 PLANES_LATE_AT = 53 * KIB
-RAW_AT = {(0, None): 55 * KIB, (1, None): 0, (2, None): 17 * KIB, (3, 0): 55 * KIB, (3, 1): 63 * KIB}
-SCALAR_COLUMNS = {(3, 0): 256, (3, 1): 384}
+RAW_AT = {
+    (0, None): 55 * KIB,
+    (1, None): 0,
+    (2, 0): 17 * KIB,
+    (3, 0): 25 * KIB,
+    (2, 1): 55 * KIB,
+    (3, 1): 63 * KIB,
+}
+SCALAR_COLUMNS = {(2, 0): 256, (3, 0): 256, (1, 1): 256, (2, 1): 384, (3, 1): 384}
+GATE_BYTES = 4 * HALF
+GROUPED_AT = {(2, 1): 0, (3, 1): 4 * GATE_BYTES}
 
 
 def tile_list_tabglu_tm_none_kernel(tc, tab, w4_words, w4_scales, w8, offs, out):
@@ -38,6 +47,7 @@ def tile_list_tabglu_tm_none_kernel(tc, tab, w4_words, w4_scales, w8, offs, out)
         shared = ctx.enter_context(tc.tile_pool(name="shared", bufs=1))
         stage = ctx.enter_context(tc.tile_pool(name="stage", bufs=5))
         outs = ctx.enter_context(tc.tile_pool(name="outs", bufs=6))
+        gating = ctx.enter_context(tc.tile_pool(name="gating", bufs=1))
         psum = ctx.enter_context(tc.psum_pool(name="psum", bufs=8))
 
         offsets = keep.tile([P, S // 16], U16, name="offsets")
@@ -47,8 +57,6 @@ def tile_list_tabglu_tm_none_kernel(tc, tab, w4_words, w4_scales, w8, offs, out)
         nc.gpsimd.memset(warm[:], 0.0)
         warm_out = keep.tile([P, 1], F32, name="warm_out")
         nc.scalar.activation(warm_out[:], warm[:], SILU)
-        moved = keep.tile([P, (PASSES - 1) * S // 4], I32, align_bytes=64, name="moved")
-        nc.gpsimd.memset(moved[:], 0)
 
         w4_codes = {}
         w4_planes = {}
@@ -72,13 +80,13 @@ def tile_list_tabglu_tm_none_kernel(tc, tab, w4_words, w4_scales, w8, offs, out)
         table = {}
 
         def load_table(a):
-            table[a] = shared.tile([P, T], I32, align_bytes=64, offset=TABLE_AT[a], name=f"table{a}")
+            table[a] = shared.tile([P, T], I32, align_bytes=256, offset=TABLE_AT[a], name=f"table{a}")
             nc.sync.dma_start(table[a][:], tab[a, 0:words_bytes].rearrange("(p x) -> p x", p=P).bitcast(I32))
 
         load_table(0)
-        w4_first = keep.tile([P, PASSES - 1, HALF // 2], I32, align_bytes=64, name="w4_first")
+        w4_first = keep.tile([P, PASSES - 1, HALF // 2], I32, align_bytes=256, name="w4_first")
         load_w4(w4_first, 0, PASSES - 1, 0)
-        table_scales = keep.tile([P, T // 4], I32, align_bytes=64, name="table_scales")
+        table_scales = keep.tile([P, T // 4], I32, align_bytes=256, name="table_scales")
         nc.vector.memset(table_scales[:], 0)
         for q in range(4):
             nc.gpsimd.dma_start(
@@ -87,11 +95,13 @@ def tile_list_tabglu_tm_none_kernel(tc, tab, w4_words, w4_scales, w8, offs, out)
                 .rearrange("a (r t) -> a r t", r=4)
                 .bitcast(I32),
             )
-        planes_first = keep.tile([P, PASSES, HALF // 4], I32, align_bytes=64, name="planes_first")
+        moved = keep.tile([P, (PASSES - 1) * S // 4], I32, align_bytes=256, name="moved")
+        nc.gpsimd.memset(moved[:], 0)
+        planes_first = keep.tile([P, PASSES, HALF // 4], I32, align_bytes=256, name="planes_first")
         nc.vector.memset(planes_first[:], 0)
         load_planes(nc.sync, planes_first, 0)
         load_table(1)
-        picked = [keep.tile([P, S], U32, align_bytes=64, name=f"picked{a}") for a in range(PASSES)]
+        picked = [keep.tile([P, S], U32, align_bytes=256, name=f"picked{a}") for a in range(PASSES)]
 
         def gather_words(a, parts=1):
             n = S // parts
@@ -102,7 +112,7 @@ def tile_list_tabglu_tm_none_kernel(tc, tab, w4_words, w4_scales, w8, offs, out)
                 )
 
         gather_words(0)
-        picked_scales = shared.tile([P, S], U8, align_bytes=64, offset=PICKED_SCALES_AT, name="picked_scales")
+        picked_scales = shared.tile([P, S], U8, align_bytes=256, offset=PICKED_SCALES_AT, name="picked_scales")
         nc.vector.tensor_copy(picked_scales[:], table_scales[:].bitcast(U8).indirect(offsets[:]))
         for a in range(1, PASSES):
             nc.scalar.dma_start(
@@ -149,21 +159,26 @@ def tile_list_tabglu_tm_none_kernel(tc, tab, w4_words, w4_scales, w8, offs, out)
             else:
                 cols, key = slice(half * HALF, (half + 1) * HALF), f"raw{a}{half}"
             width = cols.stop - cols.start
-            raw = shared.tile([P, 4, width], F32, align_bytes=64, offset=RAW_AT[a, half], name=key)
+            raw = shared.tile([P, 4, width], F32, align_bytes=256, offset=RAW_AT[a, half], name=key)
             nc.sync.dma_start(raw[:], w8[512 * a : 512 * (a + 1), cols].rearrange("(p j) n -> p j n", j=4))
             for h in range(2) if half is None else [half]:
                 raws[a, h] = raw[:, :, h * HALF : (h + 1) * HALF] if half is None else raw[:]
 
         def quantize_w8(a, h):
             cut = SCALAR_COLUMNS.get((a, h), 0)
-            grouped = stage.tile([P, HALF, 4], BF16, align_bytes=64, name="grouped")
+            if (a, h) in GROUPED_AT:
+                grouped = gating.tile(
+                    [P, HALF, 4], BF16, align_bytes=256, offset=GROUPED_AT[a, h], name=f"grouped{a}{h}"
+                )
+            else:
+                grouped = stage.tile([P, HALF, 4], BF16, align_bytes=256, name="grouped")
             dst = grouped[:].rearrange("p (c i) t -> p c t i", i=4)
             src = raws[a, h].rearrange("p t (c i) -> p c t i", i=4)
             if cut:
                 nc.scalar.copy(dst[:, : cut // 4], src[:, : cut // 4])
             nc.vector.tensor_copy(dst[:, cut // 4 :], src[:, cut // 4 :])
-            codes = keep.tile([P, HALF], U32, align_bytes=64, name=f"w8_codes{a}{h}")
-            scales = keep.tile([P, HALF], U8, align_bytes=64, name=f"w8_scales{a}{h}")
+            codes = keep.tile([P, HALF], U32, align_bytes=256, name=f"w8_codes{a}{h}")
+            scales = keep.tile([P, HALF], U8, align_bytes=256, name=f"w8_scales{a}{h}")
             nc.vector.quantize_mx(
                 out=codes[:].bitcast(FP8X4), scales=scales[:], in_=grouped[:].rearrange("p n t -> p (n t)")
             )
@@ -172,7 +187,7 @@ def tile_list_tabglu_tm_none_kernel(tc, tab, w4_words, w4_scales, w8, offs, out)
         gates = {}
 
         def gate(acc, t, h):
-            g = keep.tile([P, HALF], F32, name=f"gate{t}{h}")
+            g = gating.tile([P, HALF], F32, align_bytes=256, offset=GATE_BYTES * (TOKENS * h + t), name=f"gate{t}{h}")
             nc.scalar.activation(g[:], acc[:], SILU)
             gates[t, h] = g
 
@@ -189,12 +204,12 @@ def tile_list_tabglu_tm_none_kernel(tc, tab, w4_words, w4_scales, w8, offs, out)
             for t in range(TOKENS):
                 mm_w4(accs[t], a, t, 0)
             if a == 1:
-                w4_late0 = shared.tile([P, 1, HALF // 2], I32, align_bytes=64, offset=W4_LATE_AT[0], name="w4_late0")
+                w4_late0 = shared.tile([P, 1, HALF // 2], I32, align_bytes=256, offset=W4_LATE_AT[0], name="w4_late0")
                 load_w4(w4_late0, 3, 4, 0)
-                w4_late1 = shared.tile([P, PASSES, HALF // 2], I32, align_bytes=64, offset=W4_LATE_AT[1], name="w4_late1")
+                w4_late1 = shared.tile([P, PASSES, HALF // 2], I32, align_bytes=256, offset=W4_LATE_AT[1], name="w4_late1")
                 load_w4(w4_late1, 0, 4, 1)
                 planes_late = shared.tile(
-                    [P, PASSES, HALF // 4], I32, align_bytes=64, offset=PLANES_LATE_AT, name="planes_late"
+                    [P, PASSES, HALF // 4], I32, align_bytes=256, offset=PLANES_LATE_AT, name="planes_late"
                 )
                 nc.vector.memset(planes_late[:], 0)
                 load_planes(nc.sync, planes_late, 1)
@@ -202,7 +217,8 @@ def tile_list_tabglu_tm_none_kernel(tc, tab, w4_words, w4_scales, w8, offs, out)
             if a == 2:
                 load_w8(1, None)
             if a == 3:
-                load_w8(2, None)
+                load_w8(2, 0)
+                load_w8(3, 0)
         for t in range(TOKENS):
             gate(accs[t], t, 0)
 
@@ -210,36 +226,47 @@ def tile_list_tabglu_tm_none_kernel(tc, tab, w4_words, w4_scales, w8, offs, out)
             if t == 3:
                 quantize_w8(0, 0)
                 quantize_w8(0, 1)
-                load_w8(3, 0)
+                load_w8(2, 1)
                 load_w8(3, 1)
             if t == 7:
                 quantize_w8(1, 0)
-                quantize_w8(1, 1)
             acc = psum.tile([P, HALF], F32, name="acc")
             for a in range(PASSES):
                 mm_w4(acc, a, t, 1)
             gate(acc, t, 1)
 
         accs = [psum.tile([P, HALF], F32, name="acc") for t in range(TOKENS)]
-        for a in range(PASSES - 1):
-            if a == 2:
-                quantize_w8(2, 0)
-                quantize_w8(2, 1)
-                quantize_w8(3, 0)
+        for a in range(2):
             for t in range(TOKENS):
                 mm_w8(accs[t], a, t, 0)
+        quantize_w8(2, 0)
+        quantize_w8(3, 0)
+        quantize_w8(1, 1)
         for t in range(TOKENS):
+            mm_w8(accs[t], 2, t, 0)
             finish(accs[t], t, 0)
-            if t == 1:
+            if t == 2:
+                quantize_w8(2, 1)
+            if t == 5:
                 quantize_w8(3, 1)
 
         waiting = []
-        for t in range(TOKENS):
+        for t in range(TOKENS - 1):
             acc = psum.tile([P, HALF], F32, name="acc")
             for a in range(PASSES - 1):
                 mm_w8(acc, a, t, 1)
             waiting.append((acc, t))
-            if len(waiting) > 2:
-                finish(*waiting.pop(0), 1)
-        while waiting:
-            finish(*waiting.pop(0), 1)
+            if t >= 2:
+                while waiting:
+                    finish(*waiting.pop(0), 1)
+        t = TOKENS - 1
+        n = HALF // 2
+        for part in range(2):
+            acc = psum.tile([P, n], F32, name="acc")
+            cols = slice(part * n, (part + 1) * n)
+            for a in range(PASSES):
+                codes, scales = w8_codes[a, 1]
+                multiply(acc, a, t, codes[:, cols].bitcast(FP8X4), scales[:, cols])
+            res = outs.tile([P, n], F32, name="res")
+            nc.vector.tensor_tensor(res[:], acc[:], gates[t, 1][:, cols], MULT)
+            nc.sync.dma_start(out[t * P : (t + 1) * P, HALF + part * n : HALF + (part + 1) * n], res[:])

from contextlib import ExitStack

import concourse.mybir as mybir

K, M, T, S = 2048, 1024, 4096, 1024
FLOPS = 2 * 2 * K * M * S

F32 = mybir.dt.float32
BF16 = mybir.dt.bfloat16
I32 = mybir.dt.int32
U32 = mybir.dt.uint32
U16 = mybir.dt.uint16
U8 = mybir.dt.uint8
FP8X4 = mybir.dt.float8_e4m3fn_x4
FP4X4 = mybir.dt.float4_e2m1fn_x4
SILU = mybir.ActivationFunctionType.Silu
MULT = mybir.AluOpType.mult

P = 128
PASSES = K // 512
HALF = 512
TOKENS = S // P
KIB = 1024
TABLE_AT = [15 * KIB, 48 * KIB, 0, 17 * KIB]
PICKED_SCALES_AT = 16 * KIB
W4_LATE_AT = [48 * KIB, 49 * KIB]
PLANES_LATE_AT = 53 * KIB
RAW_AT = {
    (0, None): 55 * KIB,
    (1, None): 0,
    (2, 0): 17 * KIB,
    (3, 0): 25 * KIB,
    (2, 1): 55 * KIB,
    (3, 1): 63 * KIB,
}
SCALAR_COLUMNS = {(2, 0): 256, (3, 0): 256, (1, 1): 256, (2, 1): 384, (3, 1): 384}
GATE_BYTES = 4 * HALF
GROUPED_AT = {(2, 1): 0, (3, 1): 4 * GATE_BYTES}


def tile_list_tabglu_tm_none_kernel(tc, tab, w4_words, w4_scales, w8, offs, out):
    nc = tc.nc
    words_bytes = 512 * T

    with ExitStack() as ctx:
        keep = ctx.enter_context(tc.tile_pool(name="keep", bufs=1))
        shared = ctx.enter_context(tc.tile_pool(name="shared", bufs=1))
        stage = ctx.enter_context(tc.tile_pool(name="stage", bufs=5))
        outs = ctx.enter_context(tc.tile_pool(name="outs", bufs=6))
        gating = ctx.enter_context(tc.tile_pool(name="gating", bufs=1))
        psum = ctx.enter_context(tc.psum_pool(name="psum", bufs=8))

        offsets = keep.tile([P, S // 16], U16, name="offsets")
        nc.sync.dma_start(offsets[:], offs)

        warm = keep.tile([P, 1], F32, name="warm")
        nc.gpsimd.memset(warm[:], 0.0)
        warm_out = keep.tile([P, 1], F32, name="warm_out")
        nc.scalar.activation(warm_out[:], warm[:], SILU)

        w4_codes = {}
        w4_planes = {}

        def load_w4(tile, a0, a1, h):
            nc.sync.dma_start(
                tile[:], w4_words[a0:a1, :, h * 2 * HALF : (h + 1) * 2 * HALF].rearrange("a p x -> p a x").bitcast(I32)
            )
            for a in range(a0, a1):
                w4_codes[a, h] = tile[:, a - a0, :]

        def load_planes(engine, tile, h):
            for q in range(4):
                engine.dma_start(
                    tile[32 * q : 32 * q + 4, :, :],
                    w4_scales[:, 4 * q : 4 * q + 4, h * HALF : (h + 1) * HALF].rearrange("a r n -> r a n").bitcast(I32),
                )
            for a in range(PASSES):
                w4_planes[a, h] = tile[:, a, :].bitcast(U8)

        table = {}

        def load_table(a):
            table[a] = shared.tile([P, T], I32, align_bytes=256, offset=TABLE_AT[a], name=f"table{a}")
            nc.sync.dma_start(table[a][:], tab[a, 0:words_bytes].rearrange("(p x) -> p x", p=P).bitcast(I32))

        load_table(0)
        w4_first = keep.tile([P, PASSES - 1, HALF // 2], I32, align_bytes=256, name="w4_first")
        load_w4(w4_first, 0, PASSES - 1, 0)
        table_scales = keep.tile([P, T // 4], I32, align_bytes=256, name="table_scales")
        nc.vector.memset(table_scales[:], 0)
        for q in range(4):
            nc.gpsimd.dma_start(
                table_scales[32 * q : 32 * q + 16, :],
                tab[:, words_bytes + 4 * q * T : words_bytes + (4 * q + 4) * T]
                .rearrange("a (r t) -> a r t", r=4)
                .bitcast(I32),
            )
        moved = keep.tile([P, (PASSES - 1) * S // 4], I32, align_bytes=256, name="moved")
        nc.gpsimd.memset(moved[:], 0)
        planes_first = keep.tile([P, PASSES, HALF // 4], I32, align_bytes=256, name="planes_first")
        nc.vector.memset(planes_first[:], 0)
        load_planes(nc.sync, planes_first, 0)
        load_table(1)
        picked = [keep.tile([P, S], U32, align_bytes=256, name=f"picked{a}") for a in range(PASSES)]

        def gather_words(a, parts=1):
            n = S // parts
            for i in range(parts):
                nc.vector.tensor_copy(
                    picked[a][:, i * n : (i + 1) * n],
                    table[a][:].bitcast(U32).indirect(offsets[:, i * n // 16 : (i + 1) * n // 16]),
                )

        gather_words(0)
        picked_scales = shared.tile([P, S], U8, align_bytes=256, offset=PICKED_SCALES_AT, name="picked_scales")
        nc.vector.tensor_copy(picked_scales[:], table_scales[:].bitcast(U8).indirect(offsets[:]))
        for a in range(1, PASSES):
            nc.scalar.dma_start(
                moved[0:112, (a - 1) * S // 4 : a * S // 4], picked_scales[4 * a : 4 * a + 112, :].bitcast(I32)
            )
        load_table(2)
        load_table(3)

        moved_u8 = moved[:].bitcast(U8)

        def token_operand(a, t):
            cols = slice(t * P, (t + 1) * P)
            codes = picked[a][:, cols].bitcast(FP8X4)
            if a == 0:
                return codes, picked_scales[:, cols]
            return codes, moved_u8[:, (a - 1) * S + t * P : (a - 1) * S + (t + 1) * P]

        def multiply(acc, a, t, rhs, rhs_scale):
            codes, scales = token_operand(a, t)
            nc.tensor.matmul_mx(
                out=acc[:],
                lhsT=codes,
                lhsT_scale=scales,
                rhs=rhs,
                rhs_scale=rhs_scale,
                start=(a == 0),
                stop=(a == PASSES - 1),
            )

        def mm_w4(acc, a, t, h):
            multiply(acc, a, t, w4_codes[a, h].bitcast(U8).bitcast(FP4X4), w4_planes[a, h])

        w8_codes = {}

        def mm_w8(acc, a, t, h):
            codes, scales = w8_codes[a, h]
            multiply(acc, a, t, codes[:].bitcast(FP8X4), scales[:])

        raws = {}

        def load_w8(a, half):
            if half is None:
                cols, key = slice(0, M), f"raw{a}"
            else:
                cols, key = slice(half * HALF, (half + 1) * HALF), f"raw{a}{half}"
            width = cols.stop - cols.start
            raw = shared.tile([P, 4, width], F32, align_bytes=256, offset=RAW_AT[a, half], name=key)
            nc.sync.dma_start(raw[:], w8[512 * a : 512 * (a + 1), cols].rearrange("(p j) n -> p j n", j=4))
            for h in range(2) if half is None else [half]:
                raws[a, h] = raw[:, :, h * HALF : (h + 1) * HALF] if half is None else raw[:]

        def quantize_w8(a, h):
            cut = SCALAR_COLUMNS.get((a, h), 0)
            if (a, h) in GROUPED_AT:
                grouped = gating.tile(
                    [P, HALF, 4], BF16, align_bytes=256, offset=GROUPED_AT[a, h], name=f"grouped{a}{h}"
                )
            else:
                grouped = stage.tile([P, HALF, 4], BF16, align_bytes=256, name="grouped")
            dst = grouped[:].rearrange("p (c i) t -> p c t i", i=4)
            src = raws[a, h].rearrange("p t (c i) -> p c t i", i=4)
            if cut:
                nc.scalar.copy(dst[:, : cut // 4], src[:, : cut // 4])
            nc.vector.tensor_copy(dst[:, cut // 4 :], src[:, cut // 4 :])
            codes = keep.tile([P, HALF], U32, align_bytes=256, name=f"w8_codes{a}{h}")
            scales = keep.tile([P, HALF], U8, align_bytes=256, name=f"w8_scales{a}{h}")
            nc.vector.quantize_mx(
                out=codes[:].bitcast(FP8X4), scales=scales[:], in_=grouped[:].rearrange("p n t -> p (n t)")
            )
            w8_codes[a, h] = (codes, scales)

        gates = {}

        def gate(acc, t, h):
            g = gating.tile([P, HALF], F32, align_bytes=256, offset=GATE_BYTES * (TOKENS * h + t), name=f"gate{t}{h}")
            nc.scalar.activation(g[:], acc[:], SILU)
            gates[t, h] = g

        def finish(acc, t, h):
            mm_w8(acc, PASSES - 1, t, h)
            res = outs.tile([P, HALF], F32, name="res")
            nc.vector.tensor_tensor(res[:], acc[:], gates[t, h][:], MULT)
            nc.sync.dma_start(out[t * P : (t + 1) * P, h * HALF : (h + 1) * HALF], res[:])

        accs = [psum.tile([P, HALF], F32, name="acc") for t in range(TOKENS)]
        for a in range(PASSES):
            if a > 0:
                gather_words(a, 2 if a == PASSES - 1 else 1)
            for t in range(TOKENS):
                mm_w4(accs[t], a, t, 0)
            if a == 1:
                w4_late0 = shared.tile([P, 1, HALF // 2], I32, align_bytes=256, offset=W4_LATE_AT[0], name="w4_late0")
                load_w4(w4_late0, 3, 4, 0)
                w4_late1 = shared.tile([P, PASSES, HALF // 2], I32, align_bytes=256, offset=W4_LATE_AT[1], name="w4_late1")
                load_w4(w4_late1, 0, 4, 1)
                planes_late = shared.tile(
                    [P, PASSES, HALF // 4], I32, align_bytes=256, offset=PLANES_LATE_AT, name="planes_late"
                )
                nc.vector.memset(planes_late[:], 0)
                load_planes(nc.sync, planes_late, 1)
                load_w8(0, None)
            if a == 2:
                load_w8(1, None)
            if a == 3:
                load_w8(2, 0)
                load_w8(3, 0)
        for t in range(TOKENS):
            gate(accs[t], t, 0)

        for t in range(TOKENS):
            if t == 3:
                quantize_w8(0, 0)
                quantize_w8(0, 1)
                load_w8(2, 1)
                load_w8(3, 1)
            if t == 7:
                quantize_w8(1, 0)
            acc = psum.tile([P, HALF], F32, name="acc")
            for a in range(PASSES):
                mm_w4(acc, a, t, 1)
            gate(acc, t, 1)

        accs = [psum.tile([P, HALF], F32, name="acc") for t in range(TOKENS)]
        for a in range(2):
            for t in range(TOKENS):
                mm_w8(accs[t], a, t, 0)
        quantize_w8(2, 0)
        quantize_w8(3, 0)
        quantize_w8(1, 1)
        for t in range(TOKENS):
            mm_w8(accs[t], 2, t, 0)
            finish(accs[t], t, 0)
            if t == 2:
                quantize_w8(2, 1)
            if t == 5:
                quantize_w8(3, 1)

        waiting = []
        for t in range(TOKENS - 1):
            acc = psum.tile([P, HALF], F32, name="acc")
            for a in range(PASSES - 1):
                mm_w8(acc, a, t, 1)
            waiting.append((acc, t))
            if t >= 2:
                while waiting:
                    finish(*waiting.pop(0), 1)
        t = TOKENS - 1
        n = HALF // 2
        for part in range(2):
            acc = psum.tile([P, n], F32, name="acc")
            cols = slice(part * n, (part + 1) * n)
            for a in range(PASSES):
                codes, scales = w8_codes[a, 1]
                multiply(acc, a, t, codes[:, cols].bitcast(FP8X4), scales[:, cols])
            res = outs.tile([P, n], F32, name="res")
            nc.vector.tensor_tensor(res[:], acc[:], gates[t, 1][:, cols], MULT)
            nc.sync.dma_start(out[t * P : (t + 1) * P, HALF + part * n : HALF + (part + 1) * n], res[:])
